import numpy as np
import ml_dtypes


def mxq(x, axis, fmt="e4m3"):
    dtype, down = {"e4m3": (ml_dtypes.float8_e4m3fn, 7), "e5m2": (ml_dtypes.float8_e5m2, 14)}[fmt]
    v = np.moveaxis(np.asarray(x, np.float32).astype(ml_dtypes.bfloat16).astype(np.float64), axis, -1)
    blocks = v.reshape(v.shape[:-1] + (-1, 32))
    amax = np.abs(blocks).max(-1, keepdims=True)
    byte = np.maximum(np.where(amax > 0, np.frexp(amax)[1] - 1 + 127, 0) - down, 1)
    scale = np.exp2(byte - 127.0)
    codes = (blocks / scale).astype(np.float32).astype(dtype).astype(np.float64)
    return np.moveaxis((codes * scale).reshape(v.shape), -1, axis)


WIDE = False


def mx_kscale(k):
    if not WIDE:
        return np.ones(k)
    levels = np.array([10, -10, 5, -5, 0])
    if k % 512:
        return np.exp2(np.random.permutation(np.resize(levels, k // 32))).repeat(32)
    a = np.empty((k // 512, 16))
    for p in range(k // 512):
        a[p, :8] = np.random.permutation(np.resize(levels, 8))
        for g in range(8):
            far = levels[np.abs(levels - a[p, g]) >= 10]
            a[p, g + 8] = far[np.random.randint(len(far))]
    return np.exp2(a.ravel()).repeat(32)


def f64(x):
    return np.asarray(x).astype(np.float64)


E2M1 = np.array([0.0, 0.5, 1.0, 1.5, 2.0, 3.0, 4.0, 6.0, -0.0, -0.5, -1.0, -1.5, -2.0, -3.0, -4.0, -6.0])


def pack_weight(w, fmt):
    k, n = w.shape
    w = f64(np.asarray(w, np.float32).astype(ml_dtypes.bfloat16)).reshape(k // 32, 32, n)
    amax = np.abs(w).max(1)
    if fmt == "e4m3":
        byte = np.frexp(amax)[1] - 1 + 127 - 7
    else:
        mant, ex = np.frexp(amax / 6.0)
        byte = np.where(mant > 0.5, ex, ex - 1) + 127
    byte = np.clip(np.where(amax > 0, byte, 1), 1, 254)
    scaled = (w * np.exp2(127.0 - byte)[:, None, :]).reshape(k, n).astype(np.float32)
    by_word = np.ascontiguousarray(scaled.reshape(k // 512, 128, 4, n).transpose(0, 1, 3, 2))
    if fmt == "e4m3":
        words = by_word.astype(ml_dtypes.float8_e4m3fn).view(np.uint8)
    else:
        c = by_word.astype(ml_dtypes.float4_e2m1fn).view(np.uint8) & 0xF
        words = (c[..., 0::2] | (c[..., 1::2] << 4)).reshape(k // 512, 128, 2 * n)
    return np.ascontiguousarray(words), np.ascontiguousarray(byte.astype(np.uint8).reshape(k // 512, 16, n))


def unpack_weight(words, scales, fmt):
    g, _, n = scales.shape
    words = np.ascontiguousarray(words).reshape(g, 128, n, -1)
    if fmt == "e4m3":
        vals = words.view(ml_dtypes.float8_e4m3fn).astype(np.float64)
    else:
        nib = np.empty((g, 128, n, 4), np.uint8)
        nib[..., 0::2] = words & 0xF
        nib[..., 1::2] = words >> 4
        vals = E2M1[nib]
    vals = vals * np.repeat(np.exp2(scales.astype(np.float64) - 127.0), 8, axis=1)[..., None]
    return vals.transpose(0, 1, 3, 2).reshape(g * 512, n)


def planes(y):
    n, m = y.shape
    v = y.astype(np.float32).astype(ml_dtypes.bfloat16).astype(np.float64).reshape(n // 32, 32, m)
    top = np.abs(v).max(1)
    byte = np.clip(np.where(top > 0, np.frexp(top)[1] - 1 + 127 - 7, 1), 1, 254)
    codes = (v * np.exp2(127.0 - byte)[:, None, :]).reshape(n, m).astype(np.float32).astype(ml_dtypes.float8_e4m3fn).view(np.uint8)
    words = codes.reshape(n // 512, 128, 4, m).transpose(0, 1, 3, 2)
    return np.ascontiguousarray(words), np.ascontiguousarray(byte.astype(np.uint8).reshape(n // 512, 16, m))


K, M, T = 512, 1024, 1024


def setup_inputs():
    n = np.random.standard_normal
    s = mx_kscale(K)[:, None]
    p_w4 = pack_weight(n((K, M)) / np.sqrt(K) / s, "e2m1")
    p_w8 = pack_weight(n((K, M)) / np.sqrt(K) / s, "e4m3")
    return {
        "x": (n((K, T)) * s).astype(np.float32),
        "w4_words": p_w4[0],
        "w4_scales": p_w4[1],
        "w8_words": p_w8[0],
        "w8_scales": p_w8[1],
    }


def reference(x, w4_words, w4_scales, w8_words, w8_scales):
    xa_, xb_ = mxq(np.maximum(f64(x), 0.0), 0, "e4m3"), mxq(np.maximum(-f64(x), 0.0), 0, "e4m3")
    w4_ = unpack_weight(w4_words, w4_scales, "e2m1")
    w8_ = unpack_weight(w8_words, w8_scales, "e4m3")
    y = w4_.T @ xa_ + w8_.T @ xb_
    out_0 = y
    return (out_0,) + planes(out_0)

@@ -1,0 +1,289 @@
+from contextlib import ExitStack
+
+import concourse.mybir as mybir
+
+K, M, T = 512, 1024, 1024
+FLOPS = 2 * 2 * K * M * T
+
+F32 = mybir.dt.float32
+BF16 = mybir.dt.bfloat16
+I32 = mybir.dt.int32
+U8 = mybir.dt.uint8
+FP8X4 = mybir.dt.float8_e4m3fn_x4
+FP4X4 = mybir.dt.float4_e2m1fn_x4
+ALU = mybir.AluOpType
+ACT = mybir.ActivationFunctionType
+
+P = 128
+PACK = 4
+HALF = P * PACK
+HALVES = M // HALF
+TC = 256
+CHUNKS = T // TC
+TW = 512
+SPANS = T // TW
+BANK = 512
+PSUM_BANKS = 8
+N_FP4 = 128
+W8_PLANE = 4
+PAIR = 2
+LAST_SPLIT = 352
+
+
+def tile_mix_feat_fm_crelupl_none_kernel(
+    tc, x, w4_words, w4_scales, w8_words, w8_scales, out_0, out_1, out_2
+):
+    nc = tc.nc
+    with ExitStack() as ctx:
+        sb = ctx.enter_context(tc.tile_pool(name="sb", bufs=1))
+        ps = ctx.enter_context(tc.psum_pool(name="ps", bufs=1))
+        ctx.enter_context(tc.manual_schedule())
+
+        def tiles(label, count, shape, dtype):
+            return [sb.tile(shape, dtype, name="%s%d" % (label, i), align_bytes=64) for i in range(count)]
+
+        x_raw = tiles("x_raw", CHUNKS, [P, PACK, TC], F32)
+        w4_raw = tiles("w4_raw", HALVES, [P, 2 * HALF], U8)
+        w8_raw = tiles("w8_raw", HALVES, [P, HALF], I32)
+        ws_raw = sb.tile([P, M], U8, name="ws_raw", align_bytes=64)
+        w4_dealt = tiles("w4_dealt", HALVES, [P, 2 * HALF], U8)
+        w8_dealt = tiles("w8_dealt", HALVES, [P, HALF], I32)
+        ws_dealt = tiles("ws_dealt", HALVES, [P, HALF], U8)
+        pos_bf = tiles("pos_bf", CHUNKS, [P, TC * PACK], BF16)
+        neg_bf = tiles("neg_bf", CHUNKS, [P, TC * PACK], BF16)
+        pos_codes = tiles("pos_codes", SPANS, [P, TW], I32)
+        neg_codes = tiles("neg_codes", SPANS, [P, TW], I32)
+        pos_scales = tiles("pos_scales", SPANS, [P, TW], U8)
+        neg_scales = tiles("neg_scales", SPANS, [P, TW], U8)
+        y_narrow = tiles("y_narrow", TW // TC, [P, PACK, TC], F32)
+        y_wide = tiles("y_wide", SPANS * HALVES - 1, [P, PACK, TW], F32)
+        y_bf = tiles("y_bf", SPANS * HALVES, [P, TW * PACK], BF16)
+        y_codes = tiles("y_codes", SPANS * HALVES, [P, TW], I32)
+        y_scales = sb.tile([P, HALVES * T], U8, name="y_scales", align_bytes=64)
+
+        x_rows = x.rearrange("(p j) t -> p j t", j=PACK)
+        w8_flat = w8_words[0].rearrange("p n i -> p (n i)").bitcast(I32)
+        w4_flat = w4_words[0].bitcast(I32)
+        out_rows = out_0.rearrange("(a p r) t -> a p r t", a=HALVES, r=PACK)
+        out_words = out_1.rearrange("a p t i -> a p (t i)").bitcast(I32)
+        out_scale_rows = out_2.bitcast(I32).rearrange("a q w -> q a w")
+
+        def load_x(c):
+            nc.sync.dma_start(out=x_raw[c][:], in_=x_rows[:, :, c * TC : (c + 1) * TC])
+
+        def load_words(a):
+            nc.sync.dma_start(out=w8_raw[a][:], in_=w8_flat[:, a * HALF : (a + 1) * HALF])
+            nc.sync.dma_start(out=w4_raw[a][:].bitcast(I32), in_=w4_flat[:, a * HALF // 2 : (a + 1) * HALF // 2])
+
+        def load_scales(scales, first_row):
+            for q in range(4):
+                nc.sync.dma_start(
+                    out=ws_raw[:].bitcast(I32)[32 * q + first_row : 32 * q + first_row + 4, :],
+                    in_=scales[0].bitcast(I32)[4 * q : 4 * q + 4, :],
+                )
+
+        def deal_w8(a):
+            nc.vector.tensor_copy(
+                out=w8_dealt[a][:].rearrange("p (r c i) -> p c r i", r=PACK, i=4),
+                in_=w8_raw[a][:].rearrange("p (c i r) -> p c r i", r=PACK, i=4),
+            )
+
+        def deal_w4(a):
+            nc.vector.tensor_copy(
+                out=w4_dealt[a][:].rearrange("p (r m b) -> p r m b", r=PACK, b=2),
+                in_=w4_raw[a][:].rearrange("p (m r b) -> p r m b", r=PACK, b=2),
+            )
+
+        def deal_scales(a):
+            nc.vector.tensor_copy(
+                out=ws_dealt[a][:].rearrange("p (r m) -> p r m", r=PACK),
+                in_=ws_raw[:, a * HALF : (a + 1) * HALF].rearrange("p (m r) -> p r m", r=PACK),
+            )
+
+        def rows_view(raw):
+            return raw.rearrange("p j (c i) -> p c j i", i=PAIR)
+
+        def words_view(grouped):
+            return grouped.rearrange("p (c i j) -> p c j i", i=PAIR, j=PACK)
+
+        def make_on_scalar(grouped, c, sign):
+            nc.scalar.activation(out=words_view(grouped[c][:]), in_=rows_view(x_raw[c][:]), func=ACT.Relu, scale=sign)
+
+        def make_on_vector(grouped, c, sign):
+            nc.vector.tensor_scalar(
+                out=words_view(grouped[c][:]), in0=rows_view(x_raw[c][:]),
+                scalar1=sign, scalar2=0.0, op0=ALU.mult, op1=ALU.max,
+            )
+
+        def chunk_cols(c):
+            span, part = divmod(c, TW // TC)
+            return span, slice(part * TC, (part + 1) * TC)
+
+        def quantize_feature(codes, scales, grouped, c):
+            span, cols = chunk_cols(c)
+            nc.vector.quantize_mx(out=codes[span][:, cols].bitcast(FP8X4), scales=scales[span][:, cols], in_=grouped[c][:])
+
+        def quantize_neg(c):
+            quantize_feature(neg_codes, neg_scales, neg_bf, c)
+
+        def quantize_pos(c):
+            quantize_feature(pos_codes, pos_scales, pos_bf, c)
+
+        banks = []
+
+        def new_bank():
+            bank = ps.tile([P, BANK], F32, name="bank%d" % (len(banks) % PSUM_BANKS))
+            banks.append(bank)
+            return bank
+
+        def row_sum(out, a, r, span, t0, width, n_fp4):
+            cols = slice(r * P, (r + 1) * P)
+            nc.tensor.matmul_mx(
+                out=out,
+                lhsT=w8_dealt[a][:, cols].bitcast(FP8X4),
+                lhsT_scale=ws_dealt[a][W8_PLANE:P, cols],
+                rhs=neg_codes[span][:, t0 : t0 + width].bitcast(FP8X4),
+                rhs_scale=neg_scales[span][:, t0 : t0 + width],
+                start=True, stop=False,
+            )
+            for n0 in range(0, width, n_fp4):
+                nc.tensor.matmul_mx(
+                    out=out[:, n0 : n0 + n_fp4],
+                    lhsT=w4_dealt[a][:, 2 * r * P : 2 * (r + 1) * P].bitcast(FP4X4),
+                    lhsT_scale=ws_dealt[a][:, cols],
+                    rhs=pos_codes[span][:, t0 + n0 : t0 + n0 + n_fp4].bitcast(FP8X4),
+                    rhs_scale=pos_scales[span][:, t0 + n0 : t0 + n0 + n_fp4],
+                    start=False, stop=(n0 + n_fp4 == width),
+                )
+
+        def multiply_narrow(c):
+            made = []
+            for b in range(2):
+                bank = new_bank()
+                for s in range(2):
+                    row_sum(bank[:, s * TC : (s + 1) * TC], 0, 2 * b + s, 0, c * TC, TC, N_FP4)
+                made.append(bank)
+            return made
+
+        def multiply_wide(span, a):
+            made = []
+            for r in range(PACK):
+                bank = new_bank()
+                row_sum(bank[:], a, r, span, 0, TW, TW)
+                made.append(bank)
+            return made
+
+        def drain_narrow(c, made, b):
+            nc.scalar.copy(out=y_narrow[c][:, 2 * b : 2 * b + 2, :].rearrange("p s t -> p (s t)"), in_=made[b][:])
+
+        def store_narrow(c, r0, r1):
+            nc.sync.dma_start(out=out_rows[0][:, r0:r1, c * TC : (c + 1) * TC], in_=y_narrow[c][:, r0:r1, :])
+
+        def unit(span, a):
+            return span * HALVES + a
+
+        def drain_pair(span, a, made, r0):
+            y = y_wide[unit(span, a) - 1]
+            for r in (r0, r0 + 1):
+                nc.scalar.copy(out=y[:, r, :], in_=made[r][:])
+
+        def store_pair(span, a, r0):
+            y = y_wide[unit(span, a) - 1]
+            nc.sync.dma_start(out=out_rows[a][:, r0 : r0 + 2, span * TW : (span + 1) * TW], in_=y[:, r0 : r0 + 2, :])
+
+        def round_narrow(c):
+            nc.vector.tensor_copy(
+                out=words_view(y_bf[0][:, c * TC * PACK : (c + 1) * TC * PACK]), in_=rows_view(y_narrow[c][:])
+            )
+
+        def round_wide(span, a, t0, t1, copy):
+            u = unit(span, a)
+            copy(out=words_view(y_bf[u][:, t0 * PACK : t1 * PACK]), in_=rows_view(y_wide[u - 1][:, :, t0:t1]))
+
+        def quantize_result(span, a):
+            u = unit(span, a)
+            nc.vector.quantize_mx(
+                out=y_codes[u][:].bitcast(FP8X4),
+                scales=y_scales[:, a * T + span * TW : a * T + (span + 1) * TW],
+                in_=y_bf[u][:],
+            )
+
+        def store_words(span, a):
+            nc.sync.dma_start(out=out_words[a][:, span * TW : (span + 1) * TW], in_=y_codes[unit(span, a)][:])
+
+        nc.vector.memset(ws_raw[:].bitcast(I32), 0)
+        load_words(0)
+        load_scales(w4_scales, 0)
+        load_x(0)
+        load_scales(w8_scales, W8_PLANE)
+        load_x(1)
+        load_words(1)
+        load_x(2)
+        load_x(3)
+
+        deal_w8(0)
+        deal_w4(0)
+        make_on_scalar(pos_bf, 0, 1.0)
+        make_on_vector(neg_bf, 0, -1.0)
+        deal_scales(0)
+        quantize_neg(0)
+        quantize_pos(0)
+        first = multiply_narrow(0)
+        make_on_scalar(pos_bf, 1, 1.0)
+        make_on_vector(neg_bf, 1, -1.0)
+        deal_w8(1)
+        quantize_neg(1)
+        deal_w4(1)
+        quantize_pos(1)
+        deal_scales(1)
+        second = multiply_narrow(1)
+        made01 = multiply_wide(0, 1)
+
+        drain_narrow(0, first, 0)
+        store_narrow(0, 0, 2)
+        drain_narrow(0, first, 1)
+        store_narrow(0, 2, 4)
+        drain_narrow(1, second, 0)
+        drain_narrow(1, second, 1)
+        store_narrow(1, 0, 4)
+
+        make_on_vector(neg_bf, 2, -1.0)
+        make_on_vector(pos_bf, 2, 1.0)
+        quantize_neg(2)
+        make_on_vector(neg_bf, 3, -1.0)
+        quantize_pos(2)
+        make_on_vector(pos_bf, 3, 1.0)
+        quantize_neg(3)
+        round_narrow(0)
+        quantize_pos(3)
+
+        drain_pair(0, 1, made01, 0)
+        store_pair(0, 1, 0)
+        drain_pair(0, 1, made01, 2)
+        store_pair(0, 1, 2)
+        made10 = multiply_wide(1, 0)
+        round_narrow(1)
+        round_wide(0, 1, 0, TW, nc.vector.tensor_copy)
+        quantize_result(0, 0)
+        quantize_result(0, 1)
+        drain_pair(1, 0, made10, 0)
+        store_words(0, 0)
+        store_pair(1, 0, 0)
+        drain_pair(1, 0, made10, 2)
+        store_pair(1, 0, 2)
+        store_words(0, 1)
+        made11 = multiply_wide(1, 1)
+        round_wide(1, 0, 0, TW, nc.vector.tensor_copy)
+        quantize_result(1, 0)
+        drain_pair(1, 1, made11, 0)
+        store_pair(1, 1, 0)
+        drain_pair(1, 1, made11, 2)
+        store_pair(1, 1, 2)
+        store_words(1, 0)
+        round_wide(1, 1, 0, LAST_SPLIT, nc.vector.tensor_copy)
+        round_wide(1, 1, LAST_SPLIT, TW, nc.scalar.copy)
+        quantize_result(1, 1)
+        store_words(1, 1)
+        scale_words = y_scales[:].bitcast(I32).rearrange("p (a w) -> p a w", a=HALVES)
+        for q in range(4):
+            nc.sync.dma_start(out=out_scale_rows[4 * q : 4 * q + 4], in_=scale_words[32 * q : 32 * q + 4])

@@ -27,7 +27,7 @@ PSUM_BANKS = 8
 N_FP4 = 128
 W8_PLANE = 4
 PAIR = 2
-LAST_SPLIT = 352
+LAST_SPLIT = 256
 
 
 def tile_mix_feat_fm_crelupl_none_kernel(
@@ -55,10 +55,10 @@ def tile_mix_feat_fm_crelupl_none_kernel(
         neg_codes = tiles("neg_codes", SPANS, [P, TW], I32)
         pos_scales = tiles("pos_scales", SPANS, [P, TW], U8)
         neg_scales = tiles("neg_scales", SPANS, [P, TW], U8)
-        y_narrow = tiles("y_narrow", TW // TC, [P, PACK, TC], F32)
-        y_wide = tiles("y_wide", SPANS * HALVES - 1, [P, PACK, TW], F32)
-        y_bf = tiles("y_bf", SPANS * HALVES, [P, TW * PACK], BF16)
-        y_codes = tiles("y_codes", SPANS * HALVES, [P, TW], I32)
+        y_narrow = tiles("y_narrow", CHUNKS, [P, PACK, TC], F32)
+        y_wide = tiles("y_wide", SPANS, [P, PACK, TW], F32)
+        y_bf = [tiles("y_bf%d_" % a, SPANS, [P, TW * PACK], BF16) for a in range(HALVES)]
+        y_codes = tiles("y_codes", HALVES, [P, T], I32)
         y_scales = sb.tile([P, HALVES * T], U8, name="y_scales", align_bytes=64)
 
         x_rows = x.rearrange("(p j) t -> p j t", j=PACK)
@@ -66,7 +66,7 @@ def tile_mix_feat_fm_crelupl_none_kernel(
         w4_flat = w4_words[0].bitcast(I32)
         out_rows = out_0.rearrange("(a p r) t -> a p r t", a=HALVES, r=PACK)
         out_words = out_1.rearrange("a p t i -> a p (t i)").bitcast(I32)
-        out_scale_rows = out_2.bitcast(I32).rearrange("a q w -> q a w")
+        out_scale_rows = out_2.bitcast(I32).rearrange("a (q r) w -> r q a w", r=4)
 
         def load_x(c):
             nc.sync.dma_start(out=x_raw[c][:], in_=x_rows[:, :, c * TC : (c + 1) * TC])
@@ -76,11 +76,9 @@ def tile_mix_feat_fm_crelupl_none_kernel(
             nc.sync.dma_start(out=w4_raw[a][:].bitcast(I32), in_=w4_flat[:, a * HALF // 2 : (a + 1) * HALF // 2])
 
         def load_scales(scales, first_row):
-            for q in range(4):
-                nc.sync.dma_start(
-                    out=ws_raw[:].bitcast(I32)[32 * q + first_row : 32 * q + first_row + 4, :],
-                    in_=scales[0].bitcast(I32)[4 * q : 4 * q + 4, :],
-                )
+            rows = scales[0].bitcast(I32).rearrange("(q r) w -> r q w", r=4)
+            for r in range(4):
+                nc.sync.dma_start(out=ws_raw[:].bitcast(I32)[first_row + r : P : 32, :], in_=rows[r])
 
         def deal_w8(a):
             nc.vector.tensor_copy(
@@ -136,7 +134,7 @@ def tile_mix_feat_fm_crelupl_none_kernel(
             banks.append(bank)
             return bank
 
-        def row_sum(out, a, r, span, t0, width, n_fp4):
+        def pass_w8(out, a, r, span, t0, width, start):
             cols = slice(r * P, (r + 1) * P)
             nc.tensor.matmul_mx(
                 out=out,
@@ -144,32 +142,44 @@ def tile_mix_feat_fm_crelupl_none_kernel(
                 lhsT_scale=ws_dealt[a][W8_PLANE:P, cols],
                 rhs=neg_codes[span][:, t0 : t0 + width].bitcast(FP8X4),
                 rhs_scale=neg_scales[span][:, t0 : t0 + width],
-                start=True, stop=False,
+                start=start, stop=False,
             )
-            for n0 in range(0, width, n_fp4):
-                nc.tensor.matmul_mx(
-                    out=out[:, n0 : n0 + n_fp4],
-                    lhsT=w4_dealt[a][:, 2 * r * P : 2 * (r + 1) * P].bitcast(FP4X4),
-                    lhsT_scale=ws_dealt[a][:, cols],
-                    rhs=pos_codes[span][:, t0 + n0 : t0 + n0 + n_fp4].bitcast(FP8X4),
-                    rhs_scale=pos_scales[span][:, t0 + n0 : t0 + n0 + n_fp4],
-                    start=False, stop=(n0 + n_fp4 == width),
-                )
+
+        def pass_w4(out, a, r, span, t0, width, stop):
+            nc.tensor.matmul_mx(
+                out=out,
+                lhsT=w4_dealt[a][:, 2 * r * P : 2 * (r + 1) * P].bitcast(FP4X4),
+                lhsT_scale=ws_dealt[a][:, r * P : (r + 1) * P],
+                rhs=pos_codes[span][:, t0 : t0 + width].bitcast(FP8X4),
+                rhs_scale=pos_scales[span][:, t0 : t0 + width],
+                start=False, stop=stop,
+            )
+
+        def narrow_w8(c, made, b):
+            span, cols = chunk_cols(c)
+            for s in range(2):
+                pass_w8(made[b][:, s * TC : (s + 1) * TC], 0, 2 * b + s, span, cols.start, TC, s == 0)
+
+        def narrow_w4(c, made, b):
+            span, cols = chunk_cols(c)
+            for n0 in range(0, BANK, N_FP4):
+                s, t0 = divmod(n0, TC)
+                pass_w4(made[b][:, n0 : n0 + N_FP4], 0, 2 * b + s, span, cols.start + t0, N_FP4, n0 + N_FP4 == BANK)
 
         def multiply_narrow(c):
             made = []
             for b in range(2):
-                bank = new_bank()
-                for s in range(2):
-                    row_sum(bank[:, s * TC : (s + 1) * TC], 0, 2 * b + s, 0, c * TC, TC, N_FP4)
-                made.append(bank)
+                made.append(new_bank())
+                narrow_w8(c, made, b)
+                narrow_w4(c, made, b)
             return made
 
-        def multiply_wide(span, a):
+        def multiply_wide(span):
             made = []
             for r in range(PACK):
                 bank = new_bank()
-                row_sum(bank[:], a, r, span, 0, TW, TW)
+                pass_w8(bank[:], 1, r, span, 0, TW, True)
+                pass_w4(bank[:], 1, r, span, 0, TW, True)
                 made.append(bank)
             return made
 
@@ -179,37 +189,37 @@ def tile_mix_feat_fm_crelupl_none_kernel(
         def store_narrow(c, r0, r1):
             nc.sync.dma_start(out=out_rows[0][:, r0:r1, c * TC : (c + 1) * TC], in_=y_narrow[c][:, r0:r1, :])
 
-        def unit(span, a):
-            return span * HALVES + a
+        def finish_narrow(c, made):
+            for b in range(2):
+                drain_narrow(c, made, b)
+            store_narrow(c, 0, PACK)
 
-        def drain_pair(span, a, made, r0):
-            y = y_wide[unit(span, a) - 1]
-            for r in (r0, r0 + 1):
-                nc.scalar.copy(out=y[:, r, :], in_=made[r][:])
-
-        def store_pair(span, a, r0):
-            y = y_wide[unit(span, a) - 1]
-            nc.sync.dma_start(out=out_rows[a][:, r0 : r0 + 2, span * TW : (span + 1) * TW], in_=y[:, r0 : r0 + 2, :])
+        def finish_wide(span, made):
+            for r0 in range(0, PACK, 2):
+                for r in (r0, r0 + 1):
+                    nc.scalar.copy(out=y_wide[span][:, r, :], in_=made[r][:])
+                nc.sync.dma_start(
+                    out=out_rows[1][:, r0 : r0 + 2, span * TW : (span + 1) * TW], in_=y_wide[span][:, r0 : r0 + 2, :]
+                )
 
         def round_narrow(c):
+            span, cols = chunk_cols(c)
             nc.vector.tensor_copy(
-                out=words_view(y_bf[0][:, c * TC * PACK : (c + 1) * TC * PACK]), in_=rows_view(y_narrow[c][:])
+                out=words_view(y_bf[0][span][:, cols.start * PACK : cols.stop * PACK]), in_=rows_view(y_narrow[c][:])
             )
 
-        def round_wide(span, a, t0, t1, copy):
-            u = unit(span, a)
-            copy(out=words_view(y_bf[u][:, t0 * PACK : t1 * PACK]), in_=rows_view(y_wide[u - 1][:, :, t0:t1]))
+        def round_wide(span, t0, t1, copy):
+            copy(out=words_view(y_bf[1][span][:, t0 * PACK : t1 * PACK]), in_=rows_view(y_wide[span][:, :, t0:t1]))
 
-        def quantize_result(span, a):
-            u = unit(span, a)
+        def quantize_result(a, span):
             nc.vector.quantize_mx(
-                out=y_codes[u][:].bitcast(FP8X4),
+                out=y_codes[a][:, span * TW : (span + 1) * TW].bitcast(FP8X4),
                 scales=y_scales[:, a * T + span * TW : a * T + (span + 1) * TW],
-                in_=y_bf[u][:],
+                in_=y_bf[a][span][:],
             )
 
-        def store_words(span, a):
-            nc.sync.dma_start(out=out_words[a][:, span * TW : (span + 1) * TW], in_=y_codes[unit(span, a)][:])
+        def store_words(a):
+            nc.sync.dma_start(out=out_words[a], in_=y_codes[a][:])
 
         nc.vector.memset(ws_raw[:].bitcast(I32), 0)
         load_words(0)
@@ -227,25 +237,26 @@ def tile_mix_feat_fm_crelupl_none_kernel(
         make_on_vector(neg_bf, 0, -1.0)
         deal_scales(0)
         quantize_neg(0)
+        made0 = [new_bank(), new_bank()]
+        for b in range(2):
+            narrow_w8(0, made0, b)
         quantize_pos(0)
-        first = multiply_narrow(0)
+        for b in range(2):
+            narrow_w4(0, made0, b)
         make_on_scalar(pos_bf, 1, 1.0)
         make_on_vector(neg_bf, 1, -1.0)
         deal_w8(1)
         quantize_neg(1)
-        deal_w4(1)
         quantize_pos(1)
+        deal_w4(1)
         deal_scales(1)
-        second = multiply_narrow(1)
-        made01 = multiply_wide(0, 1)
+        made1 = multiply_narrow(1)
+        wide0 = multiply_wide(0)
 
-        drain_narrow(0, first, 0)
-        store_narrow(0, 0, 2)
-        drain_narrow(0, first, 1)
-        store_narrow(0, 2, 4)
-        drain_narrow(1, second, 0)
-        drain_narrow(1, second, 1)
-        store_narrow(1, 0, 4)
+        for b in range(2):
+            drain_narrow(0, made0, b)
+            store_narrow(0, 2 * b, 2 * b + 2)
+        finish_narrow(1, made1)
 
         make_on_vector(neg_bf, 2, -1.0)
         make_on_vector(pos_bf, 2, 1.0)
@@ -257,33 +268,26 @@ def tile_mix_feat_fm_crelupl_none_kernel(
         round_narrow(0)
         quantize_pos(3)
 
-        drain_pair(0, 1, made01, 0)
-        store_pair(0, 1, 0)
-        drain_pair(0, 1, made01, 2)
-        store_pair(0, 1, 2)
-        made10 = multiply_wide(1, 0)
+        made2 = multiply_narrow(2)
+        made3 = multiply_narrow(3)
+        finish_wide(0, wide0)
+        wide1 = multiply_wide(1)
+        finish_narrow(2, made2)
+        finish_narrow(3, made3)
+        finish_wide(1, wide1)
+
         round_narrow(1)
-        round_wide(0, 1, 0, TW, nc.vector.tensor_copy)
+        round_wide(0, 0, TW, nc.vector.tensor_copy)
         quantize_result(0, 0)
-        quantize_result(0, 1)
-        drain_pair(1, 0, made10, 0)
-        store_words(0, 0)
-        store_pair(1, 0, 0)
-        drain_pair(1, 0, made10, 2)
-        store_pair(1, 0, 2)
-        store_words(0, 1)
-        made11 = multiply_wide(1, 1)
-        round_wide(1, 0, 0, TW, nc.vector.tensor_copy)
+        round_narrow(2)
+        round_narrow(3)
         quantize_result(1, 0)
-        drain_pair(1, 1, made11, 0)
-        store_pair(1, 1, 0)
-        drain_pair(1, 1, made11, 2)
-        store_pair(1, 1, 2)
-        store_words(1, 0)
-        round_wide(1, 1, 0, LAST_SPLIT, nc.vector.tensor_copy)
-        round_wide(1, 1, LAST_SPLIT, TW, nc.scalar.copy)
+        quantize_result(0, 1)
+        store_words(0)
+        round_wide(1, 0, LAST_SPLIT, nc.vector.tensor_copy)
+        round_wide(1, LAST_SPLIT, TW, nc.scalar.copy)
         quantize_result(1, 1)
-        store_words(1, 1)
+        store_words(1)
         scale_words = y_scales[:].bitcast(I32).rearrange("p (a w) -> p a w", a=HALVES)
-        for q in range(4):
-            nc.sync.dma_start(out=out_scale_rows[4 * q : 4 * q + 4], in_=scale_words[32 * q : 32 * q + 4])
+        for r in range(4):
+            nc.scalar.dma_start(out=out_scale_rows[r], in_=scale_words[r:P:32])

from contextlib import ExitStack

import concourse.mybir as mybir

K, M, T = 512, 1024, 1024
FLOPS = 2 * 2 * K * M * T

F32 = mybir.dt.float32
BF16 = mybir.dt.bfloat16
I32 = mybir.dt.int32
U8 = mybir.dt.uint8
FP8X4 = mybir.dt.float8_e4m3fn_x4
FP4X4 = mybir.dt.float4_e2m1fn_x4
ALU = mybir.AluOpType
ACT = mybir.ActivationFunctionType

P = 128
PACK = 4
HALF = P * PACK
HALVES = M // HALF
TC = 256
CHUNKS = T // TC
TW = 512
SPANS = T // TW
BANK = 512
PSUM_BANKS = 8
N_FP4 = 128
W8_PLANE = 4
PAIR = 2
LAST_SPLIT = 256


def tile_mix_feat_fm_crelupl_none_kernel(
    tc, x, w4_words, w4_scales, w8_words, w8_scales, out_0, out_1, out_2
):
    nc = tc.nc
    with ExitStack() as ctx:
        sb = ctx.enter_context(tc.tile_pool(name="sb", bufs=1))
        ps = ctx.enter_context(tc.psum_pool(name="ps", bufs=1))
        ctx.enter_context(tc.manual_schedule())

        def tiles(label, count, shape, dtype):
            return [sb.tile(shape, dtype, name="%s%d" % (label, i), align_bytes=64) for i in range(count)]

        x_raw = tiles("x_raw", CHUNKS, [P, PACK, TC], F32)
        w4_raw = tiles("w4_raw", HALVES, [P, 2 * HALF], U8)
        w8_raw = tiles("w8_raw", HALVES, [P, HALF], I32)
        ws_raw = sb.tile([P, M], U8, name="ws_raw", align_bytes=64)
        w4_dealt = tiles("w4_dealt", HALVES, [P, 2 * HALF], U8)
        w8_dealt = tiles("w8_dealt", HALVES, [P, HALF], I32)
        ws_dealt = tiles("ws_dealt", HALVES, [P, HALF], U8)
        pos_bf = tiles("pos_bf", CHUNKS, [P, TC * PACK], BF16)
        neg_bf = tiles("neg_bf", CHUNKS, [P, TC * PACK], BF16)
        pos_codes = tiles("pos_codes", SPANS, [P, TW], I32)
        neg_codes = tiles("neg_codes", SPANS, [P, TW], I32)
        pos_scales = tiles("pos_scales", SPANS, [P, TW], U8)
        neg_scales = tiles("neg_scales", SPANS, [P, TW], U8)
        y_narrow = tiles("y_narrow", CHUNKS, [P, PACK, TC], F32)
        y_wide = tiles("y_wide", SPANS, [P, PACK, TW], F32)
        y_bf = [tiles("y_bf%d_" % a, SPANS, [P, TW * PACK], BF16) for a in range(HALVES)]
        y_codes = tiles("y_codes", HALVES, [P, T], I32)
        y_scales = sb.tile([P, HALVES * T], U8, name="y_scales", align_bytes=64)

        x_rows = x.rearrange("(p j) t -> p j t", j=PACK)
        w8_flat = w8_words[0].rearrange("p n i -> p (n i)").bitcast(I32)
        w4_flat = w4_words[0].bitcast(I32)
        out_rows = out_0.rearrange("(a p r) t -> a p r t", a=HALVES, r=PACK)
        out_words = out_1.rearrange("a p t i -> a p (t i)").bitcast(I32)
        out_scale_rows = out_2.bitcast(I32).rearrange("a (q r) w -> r q a w", r=4)

        def load_x(c):
            nc.sync.dma_start(out=x_raw[c][:], in_=x_rows[:, :, c * TC : (c + 1) * TC])

        def load_words(a):
            nc.sync.dma_start(out=w8_raw[a][:], in_=w8_flat[:, a * HALF : (a + 1) * HALF])
            nc.sync.dma_start(out=w4_raw[a][:].bitcast(I32), in_=w4_flat[:, a * HALF // 2 : (a + 1) * HALF // 2])

        def load_scales(scales, first_row):
            rows = scales[0].bitcast(I32).rearrange("(q r) w -> r q w", r=4)
            for r in range(4):
                nc.sync.dma_start(out=ws_raw[:].bitcast(I32)[first_row + r : P : 32, :], in_=rows[r])

        def deal_w8(a):
            nc.vector.tensor_copy(
                out=w8_dealt[a][:].rearrange("p (r c i) -> p c r i", r=PACK, i=4),
                in_=w8_raw[a][:].rearrange("p (c i r) -> p c r i", r=PACK, i=4),
            )

        def deal_w4(a):
            nc.vector.tensor_copy(
                out=w4_dealt[a][:].rearrange("p (r m b) -> p r m b", r=PACK, b=2),
                in_=w4_raw[a][:].rearrange("p (m r b) -> p r m b", r=PACK, b=2),
            )

        def deal_scales(a):
            nc.vector.tensor_copy(
                out=ws_dealt[a][:].rearrange("p (r m) -> p r m", r=PACK),
                in_=ws_raw[:, a * HALF : (a + 1) * HALF].rearrange("p (m r) -> p r m", r=PACK),
            )

        def rows_view(raw):
            return raw.rearrange("p j (c i) -> p c j i", i=PAIR)

        def words_view(grouped):
            return grouped.rearrange("p (c i j) -> p c j i", i=PAIR, j=PACK)

        def make_on_scalar(grouped, c, sign):
            nc.scalar.activation(out=words_view(grouped[c][:]), in_=rows_view(x_raw[c][:]), func=ACT.Relu, scale=sign)

        def make_on_vector(grouped, c, sign):
            nc.vector.tensor_scalar(
                out=words_view(grouped[c][:]), in0=rows_view(x_raw[c][:]),
                scalar1=sign, scalar2=0.0, op0=ALU.mult, op1=ALU.max,
            )

        def chunk_cols(c):
            span, part = divmod(c, TW // TC)
            return span, slice(part * TC, (part + 1) * TC)

        def quantize_feature(codes, scales, grouped, c):
            span, cols = chunk_cols(c)
            nc.vector.quantize_mx(out=codes[span][:, cols].bitcast(FP8X4), scales=scales[span][:, cols], in_=grouped[c][:])

        def quantize_neg(c):
            quantize_feature(neg_codes, neg_scales, neg_bf, c)

        def quantize_pos(c):
            quantize_feature(pos_codes, pos_scales, pos_bf, c)

        banks = []

        def new_bank():
            bank = ps.tile([P, BANK], F32, name="bank%d" % (len(banks) % PSUM_BANKS))
            banks.append(bank)
            return bank

        def pass_w8(out, a, r, span, t0, width, start):
            cols = slice(r * P, (r + 1) * P)
            nc.tensor.matmul_mx(
                out=out,
                lhsT=w8_dealt[a][:, cols].bitcast(FP8X4),
                lhsT_scale=ws_dealt[a][W8_PLANE:P, cols],
                rhs=neg_codes[span][:, t0 : t0 + width].bitcast(FP8X4),
                rhs_scale=neg_scales[span][:, t0 : t0 + width],
                start=start, stop=False,
            )

        def pass_w4(out, a, r, span, t0, width, stop):
            nc.tensor.matmul_mx(
                out=out,
                lhsT=w4_dealt[a][:, 2 * r * P : 2 * (r + 1) * P].bitcast(FP4X4),
                lhsT_scale=ws_dealt[a][:, r * P : (r + 1) * P],
                rhs=pos_codes[span][:, t0 : t0 + width].bitcast(FP8X4),
                rhs_scale=pos_scales[span][:, t0 : t0 + width],
                start=False, stop=stop,
            )

        def narrow_w8(c, made, b):
            span, cols = chunk_cols(c)
            for s in range(2):
                pass_w8(made[b][:, s * TC : (s + 1) * TC], 0, 2 * b + s, span, cols.start, TC, s == 0)

        def narrow_w4(c, made, b):
            span, cols = chunk_cols(c)
            for n0 in range(0, BANK, N_FP4):
                s, t0 = divmod(n0, TC)
                pass_w4(made[b][:, n0 : n0 + N_FP4], 0, 2 * b + s, span, cols.start + t0, N_FP4, n0 + N_FP4 == BANK)

        def multiply_narrow(c):
            made = []
            for b in range(2):
                made.append(new_bank())
                narrow_w8(c, made, b)
                narrow_w4(c, made, b)
            return made

        def multiply_wide(span):
            made = []
            for r in range(PACK):
                bank = new_bank()
                pass_w8(bank[:], 1, r, span, 0, TW, True)
                pass_w4(bank[:], 1, r, span, 0, TW, True)
                made.append(bank)
            return made

        def drain_narrow(c, made, b):
            nc.scalar.copy(out=y_narrow[c][:, 2 * b : 2 * b + 2, :].rearrange("p s t -> p (s t)"), in_=made[b][:])

        def store_narrow(c, r0, r1):
            nc.sync.dma_start(out=out_rows[0][:, r0:r1, c * TC : (c + 1) * TC], in_=y_narrow[c][:, r0:r1, :])

        def finish_narrow(c, made):
            for b in range(2):
                drain_narrow(c, made, b)
            store_narrow(c, 0, PACK)

        def finish_wide(span, made):
            for r0 in range(0, PACK, 2):
                for r in (r0, r0 + 1):
                    nc.scalar.copy(out=y_wide[span][:, r, :], in_=made[r][:])
                nc.sync.dma_start(
                    out=out_rows[1][:, r0 : r0 + 2, span * TW : (span + 1) * TW], in_=y_wide[span][:, r0 : r0 + 2, :]
                )

        def round_narrow(c):
            span, cols = chunk_cols(c)
            nc.vector.tensor_copy(
                out=words_view(y_bf[0][span][:, cols.start * PACK : cols.stop * PACK]), in_=rows_view(y_narrow[c][:])
            )

        def round_wide(span, t0, t1, copy):
            copy(out=words_view(y_bf[1][span][:, t0 * PACK : t1 * PACK]), in_=rows_view(y_wide[span][:, :, t0:t1]))

        def quantize_result(a, span):
            nc.vector.quantize_mx(
                out=y_codes[a][:, span * TW : (span + 1) * TW].bitcast(FP8X4),
                scales=y_scales[:, a * T + span * TW : a * T + (span + 1) * TW],
                in_=y_bf[a][span][:],
            )

        def store_words(a):
            nc.sync.dma_start(out=out_words[a], in_=y_codes[a][:])

        nc.vector.memset(ws_raw[:].bitcast(I32), 0)
        load_words(0)
        load_scales(w4_scales, 0)
        load_x(0)
        load_scales(w8_scales, W8_PLANE)
        load_x(1)
        load_words(1)
        load_x(2)
        load_x(3)

        deal_w8(0)
        deal_w4(0)
        make_on_scalar(pos_bf, 0, 1.0)
        make_on_vector(neg_bf, 0, -1.0)
        deal_scales(0)
        quantize_neg(0)
        made0 = [new_bank(), new_bank()]
        for b in range(2):
            narrow_w8(0, made0, b)
        quantize_pos(0)
        for b in range(2):
            narrow_w4(0, made0, b)
        make_on_scalar(pos_bf, 1, 1.0)
        make_on_vector(neg_bf, 1, -1.0)
        deal_w8(1)
        quantize_neg(1)
        quantize_pos(1)
        deal_w4(1)
        deal_scales(1)
        made1 = multiply_narrow(1)
        wide0 = multiply_wide(0)

        for b in range(2):
            drain_narrow(0, made0, b)
            store_narrow(0, 2 * b, 2 * b + 2)
        finish_narrow(1, made1)

        make_on_vector(neg_bf, 2, -1.0)
        make_on_vector(pos_bf, 2, 1.0)
        quantize_neg(2)
        make_on_vector(neg_bf, 3, -1.0)
        quantize_pos(2)
        make_on_vector(pos_bf, 3, 1.0)
        quantize_neg(3)
        round_narrow(0)
        quantize_pos(3)

        made2 = multiply_narrow(2)
        made3 = multiply_narrow(3)
        finish_wide(0, wide0)
        wide1 = multiply_wide(1)
        finish_narrow(2, made2)
        finish_narrow(3, made3)
        finish_wide(1, wide1)

        round_narrow(1)
        round_wide(0, 0, TW, nc.vector.tensor_copy)
        quantize_result(0, 0)
        round_narrow(2)
        round_narrow(3)
        quantize_result(1, 0)
        quantize_result(0, 1)
        store_words(0)
        round_wide(1, 0, LAST_SPLIT, nc.vector.tensor_copy)
        round_wide(1, LAST_SPLIT, TW, nc.scalar.copy)
        quantize_result(1, 1)
        store_words(1)
        scale_words = y_scales[:].bitcast(I32).rearrange("p (a w) -> p a w", a=HALVES)
        for r in range(4):
            nc.scalar.dma_start(out=out_scale_rows[r], in_=scale_words[r:P:32])
